import numpy as np
import ml_dtypes


def mxq(x, axis, fmt="e4m3"):
    dtype, down = {"e4m3": (ml_dtypes.float8_e4m3fn, 7), "e5m2": (ml_dtypes.float8_e5m2, 14)}[fmt]
    v = np.moveaxis(np.asarray(x, np.float32).astype(ml_dtypes.bfloat16).astype(np.float64), axis, -1)
    blocks = v.reshape(v.shape[:-1] + (-1, 32))
    amax = np.abs(blocks).max(-1, keepdims=True)
    byte = np.maximum(np.where(amax > 0, np.frexp(amax)[1] - 1 + 127, 0) - down, 1)
    scale = np.exp2(byte - 127.0)
    codes = (blocks / scale).astype(np.float32).astype(dtype).astype(np.float64)
    return np.moveaxis((codes * scale).reshape(v.shape), -1, axis)


WIDE = False


def mx_kscale(k):
    if not WIDE:
        return np.ones(k)
    levels = np.array([10, -10, 5, -5, 0])
    if k % 512:
        return np.exp2(np.random.permutation(np.resize(levels, k // 32))).repeat(32)
    a = np.empty((k // 512, 16))
    for p in range(k // 512):
        a[p, :8] = np.random.permutation(np.resize(levels, 8))
        for g in range(8):
            far = levels[np.abs(levels - a[p, g]) >= 10]
            a[p, g + 8] = far[np.random.randint(len(far))]
    return np.exp2(a.ravel()).repeat(32)


BF16 = ml_dtypes.bfloat16


def bf(x):
    return np.asarray(x, np.float32).astype(BF16)


def f64(x):
    return np.asarray(x).astype(np.float64)


E2M1 = np.array([0.0, 0.5, 1.0, 1.5, 2.0, 3.0, 4.0, 6.0, -0.0, -0.5, -1.0, -1.5, -2.0, -3.0, -4.0, -6.0])


def pack_weight(w, fmt):
    k, n = w.shape
    w = f64(bf(w)).reshape(k // 32, 32, n)
    amax = np.abs(w).max(1)
    if fmt == "e4m3":
        byte = np.frexp(amax)[1] - 1 + 127 - 7
    else:
        mant, ex = np.frexp(amax / 6.0)
        byte = np.where(mant > 0.5, ex, ex - 1) + 127
    byte = np.clip(np.where(amax > 0, byte, 1), 1, 254)
    scaled = (w * np.exp2(127.0 - byte)[:, None, :]).reshape(k, n).astype(np.float32)
    by_word = np.ascontiguousarray(scaled.reshape(k // 512, 128, 4, n).transpose(0, 1, 3, 2))
    if fmt == "e4m3":
        words = by_word.astype(ml_dtypes.float8_e4m3fn).view(np.uint8)
    else:
        c = by_word.astype(ml_dtypes.float4_e2m1fn).view(np.uint8) & 0xF
        words = c[..., 0::2] | (c[..., 1::2] << 4)
    return np.ascontiguousarray(words), np.ascontiguousarray(byte.astype(np.uint8).reshape(k // 512, 16, n))


def unpack_weight(words, scales, fmt):
    g, p, n, _ = words.shape
    if fmt == "e4m3":
        vals = np.ascontiguousarray(words).view(ml_dtypes.float8_e4m3fn).astype(np.float64)
    else:
        nib = np.empty((g, p, n, 4), np.uint8)
        nib[..., 0::2] = words & 0xF
        nib[..., 1::2] = words >> 4
        vals = E2M1[nib]
    vals = vals * np.repeat(np.exp2(scales.astype(np.float64) - 127.0), 8, axis=1)[..., None]
    return vals.transpose(0, 1, 3, 2).reshape(g * 512, n)
def pack4(w):
    words, scales = pack_weight(w, "e2m1")
    return words.reshape(words.shape[0], 128, -1), scales


def unpack4(words, scales):
    return unpack_weight(words.reshape(words.shape[0], 128, -1, 2), scales, "e2m1")


K, V, D, T = 1024, 1536, 1024, 1024


def draw0():
    s, c, u = mx_kscale(K), mx_kscale(D), mx_kscale(V)
    sim = np.random.standard_normal((V, K))
    prior = 1 + 0.1 * np.random.standard_normal(K)
    rnorm = 1 / np.sqrt(np.mean((np.exp(sim) * prior) ** 2, axis=1))
    emb = np.random.standard_normal((K, D)) / np.sqrt(K)
    hid = np.random.standard_normal((T, D)) / np.sqrt(D)
    back = np.random.standard_normal((V, K)) / np.sqrt(V)
    back_words, back_scales = pack4(back / u[:, None])
    return {"sim": bf(sim),
            "prior": bf(prior * s),
            "emb": bf(emb / s[:, None] * c),
            "rnorm": bf(rnorm * u),
            "hid": bf(hid / c),
            "back_words": back_words,
            "back_scales": back_scales}


def core(sim, prior, emb, rnorm, hid, back_words, back_scales):
    a = np.exp(f64(sim)) * f64(prior)
    e = (mxq(a, 1, "e4m3") @ mxq(f64(emb), 0, "e4m3")) * f64(rnorm)[:, None]
    logits = mxq(f64(hid), 1, "e4m3") @ mxq(e, 1, "e4m3").T
    rebuilt = unpack4(back_words, back_scales).T @ mxq(e, 0, "e4m3")
    return logits, rebuilt


def e4m3fn_bytes(y):
    return np.clip(np.asarray(y, np.float64), -448.0, 448.0).astype(np.float32).astype(ml_dtypes.float8_e4m3fn).view(np.uint8)


def e4m3fn_values(b):
    return np.asarray(b, np.uint8).view(ml_dtypes.float8_e4m3fn).astype(np.float64)


def setup_inputs():
    d = draw0()
    x0 = np.asarray(d['hid']).astype(np.float64)
    s = (np.max(np.abs(x0), axis=(0,), keepdims=True) / 448.0).astype(np.float32)
    out = {}
    for k, v in d.items():
        if k == 'hid':
            out['hid_bytes'] = e4m3fn_bytes(x0 / s.astype(np.float64))
            out['hid_scale'] = s
        else:
            out[k] = v
    return out


def reference(sim, prior, emb, rnorm, hid_bytes, hid_scale, back_words, back_scales):
    return core(sim, prior, emb, rnorm, e4m3fn_values(hid_bytes) * hid_scale.astype(np.float64), back_words, back_scales)

@@ -1,0 +1,404 @@
+from contextlib import ExitStack
+
+import concourse.mybir as mybir
+from concourse.masks import make_identity
+
+F32 = mybir.dt.float32
+BF16 = mybir.dt.bfloat16
+I32 = mybir.dt.int32
+U32 = mybir.dt.uint32
+U8 = mybir.dt.uint8
+FP8 = mybir.dt.float8_e4m3fn
+FP8X4 = mybir.dt.float8_e4m3fn_x4
+FP4X4 = mybir.dt.float4_e2m1fn_x4
+MULT = mybir.AluOpType.mult
+EXP = mybir.ActivationFunctionType.Exp
+COPY = mybir.ActivationFunctionType.Copy
+
+P = 128
+PACK = 4
+K, V, D, T = 1024, 1536, 1024, 1024
+PASS = P * PACK
+V_CHUNKS = V // PASS
+K_PASSES = K // PASS
+D_PASSES = D // PASS
+T_TILES = T // P
+K_TILES = K // P
+FLOPS = 2 * V * K * D + 2 * T * D * V + 2 * K * V * D
+
+
+def tile_tokenizer_swap_embed_s8_kernel(
+    tc, sim, prior, emb, rnorm, hid_bytes, hid_scale, back_words, back_scales, out_0, out_1
+):
+    nc = tc.nc
+    with ExitStack() as ctx:
+        const = ctx.enter_context(tc.tile_pool(name="const", bufs=1))
+        work = ctx.enter_context(tc.tile_pool(name="work", bufs=3))
+        turn_psum = ctx.enter_context(tc.psum_pool(name="turn_psum", bufs=3))
+        mx_psum = ctx.enter_context(tc.psum_pool(name="mx_psum", bufs=5))
+        ctx.enter_context(tc.manual_schedule())
+
+        ident = const.tile([P, P], F32, name="ident")
+        make_identity(nc, ident[:])
+        warm = const.tile([P, 1], F32, name="warm")
+        nc.vector.memset(warm[:], 0.0)
+        nc.scalar.activation(out=warm[:], in_=warm[:], func=EXP)
+
+        prior_sb = const.tile([P, K_PASSES, PACK], BF16, name="prior_sb")
+        rnorm_bf = const.tile([P, V_CHUNKS, PACK], BF16, name="rnorm_bf")
+        rnorm_sb = const.tile([P, V_CHUNKS * PACK], F32, name="rnorm_sb")
+        nc.scalar.dma_start(out=prior_sb[:], in_=prior.rearrange("(g p t) -> p g t", p=P, t=PACK))
+        nc.scalar.dma_start(out=rnorm_bf[:], in_=rnorm.rearrange("(h m t) -> m h t", m=P, t=PACK))
+        nc.vector.tensor_copy(out=rnorm_sb[:], in_=rnorm_bf[:].rearrange("m h t -> m (h t)"))
+
+        sim_sb, emb_sb = {}, {}
+
+        def load_sim(h, tp):
+            sim_t = const.tile([P, 2, K], BF16, name=f"sim_{h}_{tp}")
+            src = sim[PASS * h : PASS * (h + 1), :].rearrange("(m t) k -> m t k", t=PACK)
+            nc.sync.dma_start(out=sim_t[:], in_=src[:, 2 * tp : 2 * tp + 2, :])
+            sim_sb[h, tp] = sim_t
+
+        def load_emb(g, dh):
+            emb_t = const.tile([P, PACK, PASS], BF16, name=f"emb_{g}_{dh}")
+            src = emb[PASS * g : PASS * (g + 1), :].rearrange("(p j) d -> p j d", j=PACK)
+            nc.sync.dma_start(out=emb_t[:], in_=src[:, :, PASS * dh : PASS * (dh + 1)])
+            emb_sb[g, dh] = emb_t
+
+        scale_sb = const.tile([P, D], F32, name="scale_sb")
+        hid_codes_in = const.tile([P, T_TILES, D], U8, name="hid_codes_in")
+        b_words = const.tile([P, V_CHUNKS, 2 * K], U8, name="b_words", align_bytes=64)
+        b_scales = const.tile([P, V_CHUNKS, K], U8, name="b_scales", align_bytes=64)
+        nc.gpsimd.memset(b_scales[:].rearrange("p h k -> p (h k)").bitcast(I32), 0)
+
+        def load_hid(half):
+            t4 = T_TILES // 2
+            src = hid_bytes.rearrange("(r T) d -> r T d", T=T_TILES)
+            nc.sync.dma_start(out=hid_codes_in[:, t4 * half : t4 * (half + 1), :], in_=src[:, t4 * half : t4 * (half + 1), :])
+
+        def load_back():
+            nc.sync.dma_start(out=b_words[:], in_=back_words.rearrange("h p w -> p h w"))
+            src = back_scales.bitcast(I32).rearrange("h q k -> q h k")
+            for q in range(4):
+                nc.sync.dma_start(
+                    out=b_scales[32 * q : 32 * q + 4, :, :].bitcast(I32), in_=src[4 * q : 4 * q + 4, :, :]
+                )
+
+        load_sim(0, 0)
+        load_emb(0, 0)
+        load_sim(0, 1)
+        load_emb(1, 0)
+        load_emb(0, 1)
+        load_emb(1, 1)
+        for h in range(1, V_CHUNKS):
+            for tp in range(2):
+                load_sim(h, tp)
+        load_back()
+        nc.sync.dma_start(out=scale_sb[:], in_=hid_scale.rearrange("o k -> (o k)").partition_broadcast(P))
+        load_hid(0)
+        load_hid(1)
+
+        emb_codes = const.tile([P, K_PASSES, D], U32, name="emb_codes", align_bytes=64)
+        emb_planes = const.tile([P, K_PASSES, D], U8, name="emb_planes", align_bytes=64)
+        hid_codes = const.tile([P, D_PASSES, T], U32, name="hid_codes", align_bytes=64)
+        hid_planes = const.tile([P, D_PASSES, T], U8, name="hid_planes", align_bytes=64)
+        h_codes = const.tile([P, V_CHUNKS, D], U32, name="h_codes", align_bytes=64)
+        h_planes = const.tile([P, V_CHUNKS, D], U8, name="h_planes", align_bytes=64)
+        a_codes, a_planes, g_codes, g_planes = {}, {}, {}, {}
+        def a_tiles(h):
+            a_codes[h] = work.tile([P, K_PASSES, PASS], U32, name="a_codes", bufs=2, align_bytes=64)
+            a_planes[h] = work.tile([P, K_PASSES, PASS], U8, name="a_planes", bufs=2, align_bytes=64)
+
+        for h in range(V_CHUNKS):
+            g_codes[h] = const.tile([P, D_PASSES, PASS], U32, name=f"g_codes_{h}", align_bytes=64)
+            g_planes[h] = const.tile([P, D_PASSES, PASS], U8, name=f"g_planes_{h}", align_bytes=64)
+
+        copiers = {"S": nc.scalar.copy, "V": nc.vector.tensor_copy}
+        tiles = {}
+
+        def quantize(src, codes, planes):
+            nc.vector.quantize_mx(out=codes.bitcast(FP8X4), scales=planes, in_=src[:].rearrange("p c t -> p (c t)"))
+
+        def sim_turn(h, tp, g):
+            bank = turn_psum.tile([P, PASS], F32, name="turn")
+            for tt in range(2):
+                words = sim_sb[h, tp][:, tt, :].bitcast(F32)
+                for u in range(2):
+                    nc.tensor.transpose(
+                        bank[:, 256 * u + P * tt : 256 * u + P * (tt + 1)], words[:, 256 * g + u : 256 * (g + 1) : 2], ident[:]
+                    )
+            ex = work.tile([P, 256, PACK], F32, name="ex")
+            nc.scalar.activation(
+                out=ex[:].rearrange("p c (u e) -> p c u e", u=2),
+                in_=bank[:].bitcast(BF16).rearrange("p (u c e) -> p c u e", u=2, e=2),
+                func=EXP,
+            )
+            tiles["ex", h, tp, g] = ex
+
+        def a_mul(h, tp, g):
+            ag = work.tile([P, 256, PACK], BF16, name="ag", align_bytes=64)
+            nc.vector.tensor_tensor(
+                out=ag[:],
+                in0=tiles["ex", h, tp, g][:],
+                in1=prior_sb[:, g, :].unsqueeze(1).to_broadcast([P, 256, PACK]),
+                op=MULT,
+            )
+            tiles["ag", h, tp, g] = ag
+
+        def a_quant(h, tp, g):
+            if h not in a_codes:
+                a_tiles(h)
+            cols = slice(256 * tp, 256 * (tp + 1))
+            quantize(tiles["ag", h, tp, g], a_codes[h][:, g, cols], a_planes[h][:, g, cols])
+
+        def emb_group(g, dh, eng):
+            eg = work.tile([P, PASS, PACK], BF16, name="eg", tag="grp", bufs=4, align_bytes=64)
+            copiers[eng](
+                out=eg[:].rearrange("p (c i) t -> p c t i", i=4), in_=emb_sb[g, dh][:].rearrange("p t (c i) -> p c t i", i=4)
+            )
+            tiles["eg", g, dh] = eg
+
+        def emb_quant(g, dh):
+            cols = slice(PASS * dh, PASS * (dh + 1))
+            quantize(tiles["eg", g, dh], emb_codes[:, g, cols], emb_planes[:, g, cols])
+
+        def hid_mul(i):
+            hs = work.tile([P, D], BF16, name="hs", bufs=8)
+            nc.vector.tensor_tensor(out=hs[:], in0=hid_codes_in[:, i, :].bitcast(FP8), in1=scale_sb[:], op=MULT)
+            tiles["hs", i] = hs
+
+        def hid_turn(pair, g, eng):
+            bank = turn_psum.tile([P, PASS], F32, name="turn")
+            for tt in range(2):
+                words = tiles["hs", 2 * pair + tt][:].bitcast(F32)
+                for u in range(2):
+                    nc.tensor.transpose(
+                        bank[:, 256 * u + P * tt : 256 * u + P * (tt + 1)], words[:, 256 * g + u : 256 * (g + 1) : 2], ident[:]
+                    )
+            hg = work.tile([P, 256, PACK], BF16, name="hidg", bufs=4, align_bytes=64)
+            copiers[eng](
+                out=hg[:].rearrange("p c t -> p (c t)").bitcast(F32).rearrange("p (c u) -> p c u", u=2),
+                in_=bank[:].rearrange("p (u c) -> p c u", u=2),
+            )
+            tiles["hidg", pair, g] = hg
+
+        def hid_quant(pair, g):
+            cols = slice(256 * pair, 256 * (pair + 1))
+            quantize(tiles["hidg", pair, g], hid_codes[:, g, cols], hid_planes[:, g, cols])
+
+        def e_mm(h, t, dh, eng="S"):
+            acc = mx_psum.tile([P, PASS], F32, name="acc")
+            rows, cols = slice(P * t, P * (t + 1)), slice(PASS * dh, PASS * (dh + 1))
+            for g in range(K_PASSES):
+                nc.tensor.matmul_mx(
+                    out=acc[:],
+                    lhsT=a_codes[h][:, g, rows].bitcast(FP8X4),
+                    lhsT_scale=a_planes[h][:, g, rows],
+                    rhs=emb_codes[:, g, cols].bitcast(FP8X4),
+                    rhs_scale=emb_planes[:, g, cols],
+                    start=(g == 0),
+                    stop=(g == K_PASSES - 1),
+                )
+            if ("ep", h, dh) not in tiles:
+                ep = work.tile([P, PACK, PASS], BF16, name=f"ep{dh}", bufs=3)
+                tiles["ep", h, dh] = ep
+            planes = tiles["ep", h, dh][:, t, :].rearrange("m (u p e) -> m u p e", u=2, e=2)
+            sums = acc[:].rearrange("m (p u e) -> m u p e", u=2, e=2)
+            norm = rnorm_sb[:, PACK * h + t : PACK * h + t + 1]
+            if eng == "S":
+                nc.scalar.activation(out=planes, in_=sums, func=COPY, scale=norm)
+            else:
+                nc.vector.tensor_scalar(out=planes, in0=sums, scalar1=norm, scalar2=None, op0=MULT)
+
+        def h_group(h, dh, eng="V"):
+            hg = work.tile([P, PASS, PACK], BF16, name="hg", tag="grp", bufs=4, align_bytes=64)
+            copiers[eng](
+                out=hg[:].rearrange("p (c i) t -> p c t i", i=4), in_=tiles["ep", h, dh][:].rearrange("p t (c i) -> p c t i", i=4)
+            )
+            tiles["hg", h, dh] = hg
+
+        def h_quant(h, dh):
+            cols = slice(PASS * dh, PASS * (dh + 1))
+            quantize(tiles["hg", h, dh], h_codes[:, h, cols], h_planes[:, h, cols])
+
+        def e_turn(h, dh, tp, eng):
+            bank = turn_psum.tile([P, PASS], F32, name="turn")
+            for tt in range(2):
+                words = tiles["ep", h, dh][:, 2 * tp + tt, :].bitcast(F32)
+                for u in range(2):
+                    nc.tensor.transpose(
+                        bank[:, 256 * u + P * tt : 256 * u + P * (tt + 1)], words[:, P * u : P * (u + 1)], ident[:]
+                    )
+            gg = work.tile([P, 256, PACK], BF16, name="gg", align_bytes=64, bufs=8)
+            copiers[eng](
+                out=gg[:].rearrange("p c t -> p (c t)").bitcast(F32).rearrange("p (c u) -> p c u", u=2),
+                in_=bank[:].rearrange("p (u c) -> p c u", u=2),
+            )
+            tiles["gg", h, dh, tp] = gg
+
+        def g_quant(h, dh, tp):
+            cols = slice(256 * tp, 256 * (tp + 1))
+            quantize(tiles["gg", h, dh, tp], g_codes[h][:, dh, cols], g_planes[h][:, dh, cols])
+
+        def logits(h, i, eng):
+            acc = mx_psum.tile([P, PASS], F32, name="acc")
+            cols = slice(P * i, P * (i + 1))
+            for g in range(D_PASSES):
+                nc.tensor.matmul_mx(
+                    out=acc[:],
+                    lhsT=hid_codes[:, g, cols].bitcast(FP8X4),
+                    lhsT_scale=hid_planes[:, g, cols],
+                    rhs=g_codes[h][:, g, :].bitcast(FP8X4),
+                    rhs_scale=g_planes[h][:, g, :],
+                    start=(g == 0),
+                    stop=(g == D_PASSES - 1),
+                )
+            lo = work.tile([P, P, PACK], F32, name="lo", tag="res", bufs=8)
+            copiers[eng](out=lo[:], in_=acc[:].rearrange("r (t m) -> r m t", t=PACK))
+            dst = out_0.rearrange("(r T) v -> T r v", T=T_TILES)[i]
+            nc.sync.dma_start(out=dst[:, PASS * h : PASS * (h + 1)], in_=lo[:].rearrange("r m t -> r (m t)"))
+
+        def rebuilt(i, dh, chunks):
+            if chunks[0] == 0:
+                tiles["reb", i, dh] = mx_psum.tile([P, PASS], F32, name="acc")
+            cols = slice(PASS * dh, PASS * (dh + 1))
+            for h in chunks:
+                nc.tensor.matmul_mx(
+                    out=tiles["reb", i, dh][:],
+                    lhsT=b_words[:, h, 2 * P * i : 2 * P * (i + 1)].bitcast(FP4X4),
+                    lhsT_scale=b_scales[:, h, P * i : P * (i + 1)],
+                    rhs=h_codes[:, h, cols].bitcast(FP8X4),
+                    rhs_scale=h_planes[:, h, cols],
+                    start=(h == 0),
+                    stop=(h == V_CHUNKS - 1),
+                )
+
+        def rebuilt_out(i, dh, eng):
+            cols = slice(PASS * dh, PASS * (dh + 1))
+            ro = work.tile([P, PASS], F32, name="ro", tag="res", bufs=8)
+            copiers[eng](
+                out=ro[:].rearrange("k (p u e) -> k p u e", u=2, e=2),
+                in_=tiles["reb", i, dh][:].rearrange("k (u p e) -> k p u e", u=2, e=2),
+            )
+            nc.sync.dma_start(out=out_1[P * i : P * (i + 1), cols], in_=ro[:])
+
+        banks = [(tp, g) for tp in range(2) for g in range(2)]
+        emb_group(0, 0, "V")
+        sim_turn(0, 0, 0)
+        sim_turn(0, 0, 1)
+        sim_turn(0, 1, 0)
+        a_mul(0, 0, 0)
+        a_mul(0, 0, 1)
+        emb_quant(0, 0)
+        emb_group(1, 0, "S")
+        a_quant(0, 0, 0)
+        sim_turn(0, 1, 1)
+        emb_group(0, 1, "V")
+        emb_quant(1, 0)
+        a_quant(0, 0, 1)
+        a_mul(0, 1, 0)
+        sim_turn(1, 0, 0)
+        a_mul(0, 1, 1)
+        emb_quant(0, 1)
+        a_quant(0, 1, 0)
+        a_quant(0, 1, 1)
+        sim_turn(1, 0, 1)
+        e_mm(0, 0, 0)
+        e_mm(0, 1, 0)
+        a_mul(1, 0, 0)
+        sim_turn(1, 1, 0)
+        e_mm(0, 2, 0)
+        e_mm(0, 3, 0)
+        a_mul(1, 0, 1)
+        a_quant(1, 0, 0)
+        emb_group(1, 1, "S")
+        sim_turn(1, 1, 1)
+        h_group(0, 0)
+        a_quant(1, 0, 1)
+        a_mul(1, 1, 0)
+        emb_quant(1, 1)
+        a_mul(1, 1, 1)
+        h_quant(0, 0)
+        e_mm(1, 0, 0)
+        e_mm(1, 1, 0)
+        a_quant(1, 1, 0)
+        e_mm(0, 0, 1)
+        a_quant(1, 1, 1)
+        e_mm(0, 1, 1)
+        sim_turn(2, 0, 0)
+        e_mm(0, 2, 1)
+        e_mm(0, 3, 1)
+        sim_turn(2, 0, 1)
+        a_mul(2, 0, 0)
+        h_group(0, 1)
+        e_mm(1, 2, 0)
+        e_mm(1, 3, 0)
+        a_mul(2, 0, 1)
+        a_quant(2, 0, 0)
+        h_quant(0, 1)
+        h_group(1, 0)
+        sim_turn(2, 1, 0)
+        e_mm(1, 0, 1)
+        e_mm(1, 1, 1)
+        a_quant(2, 0, 1)
+        a_mul(2, 1, 0)
+        h_quant(1, 0)
+        sim_turn(2, 1, 1)
+        e_mm(1, 2, 1)
+        e_mm(1, 3, 1)
+        a_quant(2, 1, 0)
+        a_mul(2, 1, 1)
+        h_group(1, 1)
+        a_quant(2, 1, 1)
+        for dh in range(2):
+            for tp in range(2):
+                e_turn(0, dh, tp, "S")
+        e_mm(2, 0, 0)
+        e_mm(2, 1, 0)
+        h_quant(1, 1)
+        e_mm(2, 2, 0)
+        e_mm(2, 3, 0)
+        h_group(2, 0)
+        for t in range(4):
+            e_mm(2, t, 1, "SV"[t % 2])
+        h_quant(2, 0)
+        h_group(2, 1)
+        OPEN = 3
+        for n in range(OPEN):
+            rebuilt(n, 0, (0, 1))
+        for dh in range(2):
+            for tp in range(2):
+                e_turn(1, dh, tp, "S")
+        hid_mul(0)
+        for n in range(16):
+            rebuilt(n % 8, n // 8, (2,) if n < OPEN else (0, 1, 2))
+            rebuilt_out(n % 8, n // 8, "SV"[n > 10 and n % 2])
+            if n == 0:
+                h_quant(2, 1)
+            if n < 7:
+                hid_mul(n + 1)
+            if n == 5:
+                for dh in range(2):
+                    for tp in range(2):
+                        e_turn(2, dh, tp, "S")
+            if n in (7, 8, 9):
+                for dh in range(2):
+                    for tp in range(2):
+                        g_quant(n - 7, dh, tp)
+            if n == 11:
+                for p in range(2):
+                    for g in range(2):
+                        hid_turn(p, g, "SV"[g])
+            if n == 13:
+                for p in range(2):
+                    for g in range(2):
+                        hid_quant(p, g)
+        for p in range(2, 4):
+            for g in range(2):
+                hid_turn(p, g, "SV"[g])
+        for p in range(2, 4):
+            for g in range(2):
+                hid_quant(p, g)
+        for h in range(3):
+            for i in range(8):
+                logits(h, i, "SV"[i % 2])

@@ -40,6 +40,8 @@ def tile_tokenizer_swap_embed_s8_kernel(
 
         ident = const.tile([P, P], F32, name="ident")
         make_identity(nc, ident[:])
+        ident_bf = const.tile([P, P], BF16, name="ident_bf")
+        make_identity(nc, ident_bf[:])
         warm = const.tile([P, 1], F32, name="warm")
         nc.vector.memset(warm[:], 0.0)
         nc.scalar.activation(out=warm[:], in_=warm[:], func=EXP)
@@ -54,7 +56,7 @@ def tile_tokenizer_swap_embed_s8_kernel(
         sim_sb, emb_sb = {}, {}
 
         def load_sim(h, tp):
-            sim_t = const.tile([P, 2, K], BF16, name=f"sim_{h}_{tp}")
+            sim_t = work.tile([P, 2, K], BF16, name="sim_t", bufs=4)
             src = sim[PASS * h : PASS * (h + 1), :].rearrange("(m t) k -> m t k", t=PACK)
             nc.sync.dma_start(out=sim_t[:], in_=src[:, 2 * tp : 2 * tp + 2, :])
             sim_sb[h, tp] = sim_t
@@ -90,13 +92,8 @@ def tile_tokenizer_swap_embed_s8_kernel(
         load_emb(1, 0)
         load_emb(0, 1)
         load_emb(1, 1)
-        for h in range(1, V_CHUNKS):
-            for tp in range(2):
-                load_sim(h, tp)
-        load_back()
-        nc.sync.dma_start(out=scale_sb[:], in_=hid_scale.rearrange("o k -> (o k)").partition_broadcast(P))
-        load_hid(0)
-        load_hid(1)
+        for tp in range(2):
+            load_sim(1, tp)
 
         emb_codes = const.tile([P, K_PASSES, D], U32, name="emb_codes", align_bytes=64)
         emb_planes = const.tile([P, K_PASSES, D], U8, name="emb_planes", align_bytes=64)
@@ -127,7 +124,7 @@ def tile_tokenizer_swap_embed_s8_kernel(
                     nc.tensor.transpose(
                         bank[:, 256 * u + P * tt : 256 * u + P * (tt + 1)], words[:, 256 * g + u : 256 * (g + 1) : 2], ident[:]
                     )
-            ex = work.tile([P, 256, PACK], F32, name="ex")
+            ex = work.tile([P, 256, PACK], F32, name="ex", bufs=5)
             nc.scalar.activation(
                 out=ex[:].rearrange("p c (u e) -> p c u e", u=2),
                 in_=bank[:].bitcast(BF16).rearrange("p (u c e) -> p c u e", u=2, e=2),
@@ -157,6 +154,27 @@ def tile_tokenizer_swap_embed_s8_kernel(
                 out=eg[:].rearrange("p (c i) t -> p c t i", i=4), in_=emb_sb[g, dh][:].rearrange("p t (c i) -> p c t i", i=4)
             )
             tiles["eg", g, dh] = eg
+
+        def emb_turn(g, dh, half, eng):
+            bank = turn_psum.tile([P, 2 * P * PACK], BF16, name="turn_bf", tag="turn")
+            for n in range(2):
+                d0 = 2 * P * half + P * n
+                nc.tensor.matmul(
+                    out=bank[:, PASS * n : PASS * (n + 1)],
+                    lhsT=ident_bf[:],
+                    rhs=emb_sb[g, dh][:, :, d0 : d0 + P].rearrange("p t d -> p d t"),
+                    start=True,
+                    stop=True,
+                )
+            if ("eg", g, dh) not in tiles:
+                eg = work.tile([P, PASS, PACK], BF16, name="eg", tag="grp", bufs=4, align_bytes=64)
+                tiles["eg", g, dh] = eg
+            copiers[eng](
+                out=tiles["eg", g, dh][:, 2 * P * half : 2 * P * (half + 1), :].rearrange("p d t -> p (d t)"), in_=bank[:]
+            )
+
+        def emb_quant2(g, dh):
+            emb_quant(g, dh)
 
         def emb_quant(g, dh):
             cols = slice(PASS * dh, PASS * (dh + 1))
@@ -283,113 +301,104 @@ def tile_tokenizer_swap_embed_s8_kernel(
             nc.sync.dma_start(out=out_1[P * i : P * (i + 1), cols], in_=ro[:])
 
         banks = [(tp, g) for tp in range(2) for g in range(2)]
-        emb_group(0, 0, "V")
+        turns = [(dh, tp) for dh in range(2) for tp in range(2)]
         sim_turn(0, 0, 0)
         sim_turn(0, 0, 1)
-        sim_turn(0, 1, 0)
+        emb_turn(0, 0, 0, "V")
+        emb_turn(0, 0, 1, "V")
         a_mul(0, 0, 0)
+        sim_turn(0, 1, 0)
+        emb_quant2(0, 0)
         a_mul(0, 0, 1)
-        emb_quant(0, 0)
-        emb_group(1, 0, "S")
-        a_quant(0, 0, 0)
         sim_turn(0, 1, 1)
-        emb_group(0, 1, "V")
-        emb_quant(1, 0)
+        for tp in range(2):
+            load_sim(2, tp)
+        load_back()
+        nc.sync.dma_start(out=scale_sb[:], in_=hid_scale.rearrange("o k -> (o k)").partition_broadcast(P))
+        load_hid(0)
+        load_hid(1)
+        a_quant(0, 0, 0)
+        emb_turn(1, 0, 0, "S")
+        emb_turn(1, 0, 1, "V")
         a_quant(0, 0, 1)
         a_mul(0, 1, 0)
+        emb_quant2(1, 0)
+        emb_turn(0, 1, 0, "S")
+        emb_turn(0, 1, 1, "V")
         sim_turn(1, 0, 0)
-        a_mul(0, 1, 1)
-        emb_quant(0, 1)
-        a_quant(0, 1, 0)
-        a_quant(0, 1, 1)
         sim_turn(1, 0, 1)
-        e_mm(0, 0, 0)
-        e_mm(0, 1, 0)
+        a_mul(0, 1, 1)
+        emb_quant2(0, 1)
+        a_quant(0, 1, 0)
+        emb_turn(1, 1, 0, "S")
+        emb_turn(1, 1, 1, "V")
+        a_quant(0, 1, 1)
         a_mul(1, 0, 0)
         sim_turn(1, 1, 0)
-        e_mm(0, 2, 0)
-        e_mm(0, 3, 0)
-        a_mul(1, 0, 1)
-        a_quant(1, 0, 0)
-        emb_group(1, 1, "S")
+        e_mm(0, 0, 0)
+        e_mm(0, 1, 0)
         sim_turn(1, 1, 1)
-        h_group(0, 0)
+        a_mul(1, 0, 1)
+        emb_quant2(1, 1)
+        a_quant(1, 0, 0)
         a_quant(1, 0, 1)
         a_mul(1, 1, 0)
-        emb_quant(1, 1)
+        for i, (tp, g) in enumerate(banks):
+            for t in range(2) if i else ():
+                e_mm(0, 2 * (i % 2) + t, i // 2)
+            sim_turn(2, tp, g)
         a_mul(1, 1, 1)
-        h_quant(0, 0)
-        e_mm(1, 0, 0)
-        e_mm(1, 1, 0)
         a_quant(1, 1, 0)
-        e_mm(0, 0, 1)
-        a_quant(1, 1, 1)
-        e_mm(0, 1, 1)
-        sim_turn(2, 0, 0)
-        e_mm(0, 2, 1)
-        e_mm(0, 3, 1)
-        sim_turn(2, 0, 1)
         a_mul(2, 0, 0)
-        h_group(0, 1)
-        e_mm(1, 2, 0)
-        e_mm(1, 3, 0)
+        a_quant(1, 1, 1)
         a_mul(2, 0, 1)
-        a_quant(2, 0, 0)
-        h_quant(0, 1)
-        h_group(1, 0)
-        sim_turn(2, 1, 0)
-        e_mm(1, 0, 1)
-        e_mm(1, 1, 1)
-        a_quant(2, 0, 1)
-        a_mul(2, 1, 0)
-        h_quant(1, 0)
-        sim_turn(2, 1, 1)
-        e_mm(1, 2, 1)
-        e_mm(1, 3, 1)
-        a_quant(2, 1, 0)
-        a_mul(2, 1, 1)
-        h_group(1, 1)
-        a_quant(2, 1, 1)
-        for dh in range(2):
-            for tp in range(2):
-                e_turn(0, dh, tp, "S")
-        e_mm(2, 0, 0)
-        e_mm(2, 1, 0)
-        h_quant(1, 1)
-        e_mm(2, 2, 0)
-        e_mm(2, 3, 0)
-        h_group(2, 0)
         for t in range(4):
-            e_mm(2, t, 1, "SV"[t % 2])
+            e_mm(1, t, 0)
+        a_quant(2, 0, 0)
+        a_mul(2, 1, 0)
+        a_quant(2, 0, 1)
+        a_mul(2, 1, 1)
+        a_quant(2, 1, 0)
+        for t in range(4):
+            e_mm(1, t, 1)
+        h_group(0, 0)
+        a_quant(2, 1, 1)
+        for t in range(4):
+            e_mm(2, t, 0)
+        h_group(0, 1)
+        h_quant(0, 0)
+        h_group(1, 0)
+        h_quant(0, 1)
+        for dh, tp in turns:
+            e_turn(0, dh, tp, "S")
+        for t in range(4):
+            e_mm(2, t, 1)
+        h_group(2, 0)
+        h_quant(1, 0)
+        h_group(1, 1)
         h_quant(2, 0)
+        for dh, tp in turns:
+            g_quant(0, dh, tp)
         h_group(2, 1)
-        OPEN = 3
-        for n in range(OPEN):
-            rebuilt(n, 0, (0, 1))
-        for dh in range(2):
-            for tp in range(2):
-                e_turn(1, dh, tp, "S")
+        h_quant(1, 1)
         hid_mul(0)
+        h_quant(2, 1)
         for n in range(16):
-            rebuilt(n % 8, n // 8, (2,) if n < OPEN else (0, 1, 2))
-            rebuilt_out(n % 8, n // 8, "SV"[n > 10 and n % 2])
-            if n == 0:
-                h_quant(2, 1)
+            rebuilt(n % 8, n // 8, (0, 1, 2))
+            rebuilt_out(n % 8, n // 8, "SV"[n > 8 and n % 2])
             if n < 7:
                 hid_mul(n + 1)
-            if n == 5:
-                for dh in range(2):
-                    for tp in range(2):
-                        e_turn(2, dh, tp, "S")
-            if n in (7, 8, 9):
-                for dh in range(2):
-                    for tp in range(2):
-                        g_quant(n - 7, dh, tp)
-            if n == 11:
+            if n in (0, 5):
+                for dh, tp in turns:
+                    e_turn(1 + (n == 5), dh, tp, "S")
+            if n in (7, 8):
+                for dh, tp in turns:
+                    g_quant(n - 6, dh, tp)
+            if n == 9:
                 for p in range(2):
                     for g in range(2):
                         hid_turn(p, g, "SV"[g])
-            if n == 13:
+            if n == 11:
                 for p in range(2):
                     for g in range(2):
                         hid_quant(p, g)

@@ -49,9 +49,13 @@ def tile_tokenizer_swap_embed_s8_kernel(
         prior_sb = const.tile([P, K_PASSES, PACK], BF16, name="prior_sb")
         rnorm_bf = const.tile([P, V_CHUNKS, PACK], BF16, name="rnorm_bf")
         rnorm_sb = const.tile([P, V_CHUNKS * PACK], F32, name="rnorm_sb")
-        nc.scalar.dma_start(out=prior_sb[:], in_=prior.rearrange("(g p t) -> p g t", p=P, t=PACK))
-        nc.scalar.dma_start(out=rnorm_bf[:], in_=rnorm.rearrange("(h m t) -> m h t", m=P, t=PACK))
-        nc.vector.tensor_copy(out=rnorm_sb[:], in_=rnorm_bf[:].rearrange("m h t -> m (h t)"))
+
+        def load_prior():
+            nc.sync.dma_start(out=prior_sb[:], in_=prior.rearrange("(g p t) -> p g t", p=P, t=PACK))
+
+        def load_rnorm():
+            nc.sync.dma_start(out=rnorm_bf[:], in_=rnorm.rearrange("(h m t) -> m h t", m=P, t=PACK))
+            nc.gpsimd.tensor_copy(out=rnorm_sb[:], in_=rnorm_bf[:].rearrange("m h t -> m (h t)"))
 
         sim_sb, emb_sb = {}, {}
 
@@ -62,7 +66,7 @@ def tile_tokenizer_swap_embed_s8_kernel(
             sim_sb[h, tp] = sim_t
 
         def load_emb(g, dh):
-            emb_t = const.tile([P, PACK, PASS], BF16, name=f"emb_{g}_{dh}")
+            emb_t = work.tile([P, PACK, PASS], BF16, name="emb_t", tag="big", bufs=4)
             src = emb[PASS * g : PASS * (g + 1), :].rearrange("(p j) d -> p j d", j=PACK)
             nc.sync.dma_start(out=emb_t[:], in_=src[:, :, PASS * dh : PASS * (dh + 1)])
             emb_sb[g, dh] = emb_t
@@ -87,11 +91,13 @@ def tile_tokenizer_swap_embed_s8_kernel(
                 )
 
         load_sim(0, 0)
+        load_prior()
         load_emb(0, 0)
         load_sim(0, 1)
         load_emb(1, 0)
         load_emb(0, 1)
         load_emb(1, 1)
+        load_rnorm()
         for tp in range(2):
             load_sim(1, tp)
 
@@ -103,12 +109,20 @@ def tile_tokenizer_swap_embed_s8_kernel(
         h_planes = const.tile([P, V_CHUNKS, D], U8, name="h_planes", align_bytes=64)
         a_codes, a_planes, g_codes, g_planes = {}, {}, {}, {}
         def a_tiles(h):
-            a_codes[h] = work.tile([P, K_PASSES, PASS], U32, name="a_codes", bufs=2, align_bytes=64)
-            a_planes[h] = work.tile([P, K_PASSES, PASS], U8, name="a_planes", bufs=2, align_bytes=64)
+            a_codes[h] = work.tile([P, K_PASSES, PASS], U32, name="a_codes", bufs=3, align_bytes=64)
+            a_planes[h] = work.tile([P, K_PASSES, PASS], U8, name="a_planes", bufs=3, align_bytes=64)
 
         for h in range(V_CHUNKS):
             g_codes[h] = const.tile([P, D_PASSES, PASS], U32, name=f"g_codes_{h}", align_bytes=64)
             g_planes[h] = const.tile([P, D_PASSES, PASS], U8, name=f"g_planes_{h}", align_bytes=64)
+
+        def late_loads():
+            for tp in range(2):
+                load_sim(2, tp)
+            load_back()
+            load_hid(0)
+            load_hid(1)
+            nc.sync.dma_start(out=scale_sb[:], in_=hid_scale.rearrange("o k -> (o k)").partition_broadcast(P))
 
         copiers = {"S": nc.scalar.copy, "V": nc.vector.tensor_copy}
         tiles = {}
@@ -181,17 +195,24 @@ def tile_tokenizer_swap_embed_s8_kernel(
             quantize(tiles["eg", g, dh], emb_codes[:, g, cols], emb_planes[:, g, cols])
 
         def hid_mul(i):
-            hs = work.tile([P, D], BF16, name="hs", bufs=8)
+            hs = work.tile([P, D], BF16, name="hs", bufs=4)
             nc.vector.tensor_tensor(out=hs[:], in0=hid_codes_in[:, i, :].bitcast(FP8), in1=scale_sb[:], op=MULT)
             tiles["hs", i] = hs
+
+        def hid_fold(i, eng):
+            hf = work.tile([P, D_PASSES, 2, P], F32, name="hf", bufs=5)
+            copiers[eng](
+                out=hf[:].rearrange("r g u p -> r g u p"),
+                in_=tiles["hs", i][:].bitcast(F32).rearrange("r (g p u) -> r g u p", g=D_PASSES, u=2),
+            )
+            tiles["hf", i] = hf
 
         def hid_turn(pair, g, eng):
             bank = turn_psum.tile([P, PASS], F32, name="turn")
             for tt in range(2):
-                words = tiles["hs", 2 * pair + tt][:].bitcast(F32)
                 for u in range(2):
                     nc.tensor.transpose(
-                        bank[:, 256 * u + P * tt : 256 * u + P * (tt + 1)], words[:, 256 * g + u : 256 * (g + 1) : 2], ident[:]
+                        bank[:, 256 * u + P * tt : 256 * u + P * (tt + 1)], tiles["hf", 2 * pair + tt][:, g, u, :], ident[:]
                     )
             hg = work.tile([P, 256, PACK], BF16, name="hidg", bufs=4, align_bytes=64)
             copiers[eng](
@@ -247,7 +268,7 @@ def tile_tokenizer_swap_embed_s8_kernel(
                     nc.tensor.transpose(
                         bank[:, 256 * u + P * tt : 256 * u + P * (tt + 1)], words[:, P * u : P * (u + 1)], ident[:]
                     )
-            gg = work.tile([P, 256, PACK], BF16, name="gg", align_bytes=64, bufs=8)
+            gg = work.tile([P, 256, PACK], BF16, name="gg", align_bytes=64, bufs=6)
             copiers[eng](
                 out=gg[:].rearrange("p c t -> p (c t)").bitcast(F32).rearrange("p (c u) -> p c u", u=2),
                 in_=bank[:].rearrange("p (u c) -> p c u", u=2),
@@ -271,10 +292,17 @@ def tile_tokenizer_swap_embed_s8_kernel(
                     start=(g == 0),
                     stop=(g == D_PASSES - 1),
                 )
-            lo = work.tile([P, P, PACK], F32, name="lo", tag="res", bufs=8)
-            copiers[eng](out=lo[:], in_=acc[:].rearrange("r (t m) -> r m t", t=PACK))
+            if ("lo", i) not in tiles:
+                lo = work.tile([P, V], F32, name="lo", tag="big", bufs=4)
+                tiles["lo", i] = lo
+            cols = slice(PASS * h, PASS * (h + 1))
+            piece = tiles["lo", i][:, cols]
+            copiers[eng](out=piece.rearrange("r (m t) -> r m t", t=PACK), in_=acc[:].rearrange("r (t m) -> r m t", t=PACK))
             dst = out_0.rearrange("(r T) v -> T r v", T=T_TILES)[i]
-            nc.sync.dma_start(out=dst[:, PASS * h : PASS * (h + 1)], in_=lo[:].rearrange("r m t -> r (m t)"))
+            if i == T_TILES - 1:
+                nc.sync.dma_start(out=dst[:, cols], in_=piece)
+            elif h == V_CHUNKS - 1:
+                nc.sync.dma_start(out=dst, in_=tiles["lo", i][:])
 
         def rebuilt(i, dh, chunks):
             if chunks[0] == 0:
@@ -293,121 +321,203 @@ def tile_tokenizer_swap_embed_s8_kernel(
 
         def rebuilt_out(i, dh, eng):
             cols = slice(PASS * dh, PASS * (dh + 1))
-            ro = work.tile([P, PASS], F32, name="ro", tag="res", bufs=8)
+            ro = work.tile([P, PASS], F32, name="ro", bufs=4)
             copiers[eng](
                 out=ro[:].rearrange("k (p u e) -> k p u e", u=2, e=2),
                 in_=tiles["reb", i, dh][:].rearrange("k (u p e) -> k p u e", u=2, e=2),
             )
             nc.sync.dma_start(out=out_1[P * i : P * (i + 1), cols], in_=ro[:])
 
-        banks = [(tp, g) for tp in range(2) for g in range(2)]
-        turns = [(dh, tp) for dh in range(2) for tp in range(2)]
+        emb_group(0, 0, "V")
         sim_turn(0, 0, 0)
-        sim_turn(0, 0, 1)
-        emb_turn(0, 0, 0, "V")
-        emb_turn(0, 0, 1, "V")
         a_mul(0, 0, 0)
+        sim_turn(0, 0, 1)
         sim_turn(0, 1, 0)
-        emb_quant2(0, 0)
         a_mul(0, 0, 1)
         sim_turn(0, 1, 1)
-        for tp in range(2):
-            load_sim(2, tp)
-        load_back()
-        nc.sync.dma_start(out=scale_sb[:], in_=hid_scale.rearrange("o k -> (o k)").partition_broadcast(P))
-        load_hid(0)
-        load_hid(1)
+        late_loads()
         a_quant(0, 0, 0)
-        emb_turn(1, 0, 0, "S")
-        emb_turn(1, 0, 1, "V")
-        a_quant(0, 0, 1)
         a_mul(0, 1, 0)
-        emb_quant2(1, 0)
-        emb_turn(0, 1, 0, "S")
-        emb_turn(0, 1, 1, "V")
-        sim_turn(1, 0, 0)
-        sim_turn(1, 0, 1)
+        emb_group(1, 0, "V")
         a_mul(0, 1, 1)
-        emb_quant2(0, 1)
+        emb_group(0, 1, "S")
+        a_quant(0, 0, 1)
+        emb_group(1, 1, "V")
         a_quant(0, 1, 0)
-        emb_turn(1, 1, 0, "S")
-        emb_turn(1, 1, 1, "V")
-        a_quant(0, 1, 1)
-        a_mul(1, 0, 0)
+        emb_quant(0, 0)
+        sim_turn(1, 0, 0)
+        emb_quant(1, 0)
+        sim_turn(1, 0, 1)
         sim_turn(1, 1, 0)
-        e_mm(0, 0, 0)
-        e_mm(0, 1, 0)
         sim_turn(1, 1, 1)
+        a_quant(0, 1, 1)
+        emb_quant(0, 1)
+        a_mul(1, 0, 0)
         a_mul(1, 0, 1)
-        emb_quant2(1, 1)
+        emb_quant(1, 1)
+        a_mul(1, 1, 0)
+        sim_turn(2, 0, 0)
         a_quant(1, 0, 0)
         a_quant(1, 0, 1)
-        a_mul(1, 1, 0)
-        for i, (tp, g) in enumerate(banks):
-            for t in range(2) if i else ():
-                e_mm(0, 2 * (i % 2) + t, i // 2)
-            sim_turn(2, tp, g)
         a_mul(1, 1, 1)
+        sim_turn(2, 0, 1)
         a_quant(1, 1, 0)
-        a_mul(2, 0, 0)
         a_quant(1, 1, 1)
+        e_mm(0, 0, 0, "S")
+        sim_turn(2, 1, 0)
+        e_mm(0, 1, 0, "S")
+        sim_turn(2, 1, 1)
+        e_mm(0, 2, 0, "V")
+        e_mm(0, 3, 0, "S")
+        a_mul(2, 0, 0)
+        e_mm(0, 0, 1, "S")
+        e_mm(0, 1, 1, "V")
+        e_mm(0, 2, 1, "S")
+        e_mm(0, 3, 1, "S")
+        e_turn(0, 0, 0, "S")
         a_mul(2, 0, 1)
-        for t in range(4):
-            e_mm(1, t, 0)
-        a_quant(2, 0, 0)
+        e_turn(0, 0, 1, "S")
+        e_turn(0, 1, 0, "S")
+        e_turn(0, 1, 1, "V")
         a_mul(2, 1, 0)
+        a_quant(2, 0, 0)
         a_quant(2, 0, 1)
         a_mul(2, 1, 1)
         a_quant(2, 1, 0)
-        for t in range(4):
-            e_mm(1, t, 1)
-        h_group(0, 0)
         a_quant(2, 1, 1)
-        for t in range(4):
-            e_mm(2, t, 0)
-        h_group(0, 1)
-        h_quant(0, 0)
-        h_group(1, 0)
-        h_quant(0, 1)
-        for dh, tp in turns:
-            e_turn(0, dh, tp, "S")
-        for t in range(4):
-            e_mm(2, t, 1)
-        h_group(2, 0)
+        e_mm(1, 0, 0, "S")
+        e_mm(1, 1, 0, "S")
+        e_mm(1, 2, 0, "S")
+        e_mm(1, 3, 0, "S")
+        e_mm(1, 0, 1, "S")
+        e_mm(1, 1, 1, "S")
+        e_mm(1, 2, 1, "S")
+        h_group(0, 0, "V")
+        h_group(0, 1, "V")
+        e_mm(1, 3, 1, "S")
+        g_quant(0, 0, 0)
+        e_mm(2, 0, 0, "S")
+        e_mm(2, 1, 0, "S")
+        g_quant(0, 0, 1)
+        h_group(1, 0, "V")
+        e_turn(1, 0, 0, "S")
+        e_mm(2, 2, 0, "S")
+        e_turn(1, 0, 1, "S")
+        e_turn(1, 1, 0, "V")
+        e_turn(1, 1, 1, "S")
+        e_mm(2, 3, 0, "S")
+        e_mm(2, 0, 1, "S")
+        g_quant(0, 1, 0)
+        h_group(2, 0, "V")
+        e_mm(2, 1, 1, "S")
         h_quant(1, 0)
-        h_group(1, 1)
+        h_quant(0, 0)
+        e_mm(2, 2, 1, "S")
         h_quant(2, 0)
-        for dh, tp in turns:
-            g_quant(0, dh, tp)
-        h_group(2, 1)
-        h_quant(1, 1)
-        hid_mul(0)
+        g_quant(1, 0, 0)
+        e_mm(2, 3, 1, "S")
+        g_quant(0, 1, 1)
+        g_quant(1, 0, 1)
+        h_group(2, 1, "V")
+        g_quant(1, 1, 0)
+        h_quant(0, 1)
+        g_quant(1, 1, 1)
+        h_group(1, 1, "V")
+        e_turn(2, 0, 0, "S")
         h_quant(2, 1)
-        for n in range(16):
-            rebuilt(n % 8, n // 8, (0, 1, 2))
-            rebuilt_out(n % 8, n // 8, "SV"[n > 8 and n % 2])
-            if n < 7:
-                hid_mul(n + 1)
-            if n in (0, 5):
-                for dh, tp in turns:
-                    e_turn(1 + (n == 5), dh, tp, "S")
-            if n in (7, 8):
-                for dh, tp in turns:
-                    g_quant(n - 6, dh, tp)
-            if n == 9:
-                for p in range(2):
-                    for g in range(2):
-                        hid_turn(p, g, "SV"[g])
-            if n == 11:
-                for p in range(2):
-                    for g in range(2):
-                        hid_quant(p, g)
-        for p in range(2, 4):
-            for g in range(2):
-                hid_turn(p, g, "SV"[g])
-        for p in range(2, 4):
-            for g in range(2):
-                hid_quant(p, g)
-        for h in range(3):
-            for i in range(8):
-                logits(h, i, "SV"[i % 2])
+        e_turn(2, 0, 1, "S")
+        h_quant(1, 1)
+        e_turn(2, 1, 0, "S")
+        hid_mul(0)
+        hid_mul(1)
+        hid_mul(2)
+        hid_mul(3)
+        e_turn(2, 1, 1, "S")
+        rebuilt(0, 0, (0, 1, 2))
+        rebuilt_out(0, 0, "S")
+        rebuilt(1, 0, (0, 1, 2))
+        rebuilt(2, 0, (0, 1, 2))
+        rebuilt(3, 0, (0, 1, 2))
+        rebuilt_out(1, 0, "S")
+        rebuilt(4, 0, (0, 1, 2))
+        rebuilt(5, 0, (0, 1, 2))
+        rebuilt(6, 0, (0, 1, 2))
+        rebuilt_out(2, 0, "S")
+        rebuilt(7, 0, (0, 1, 2))
+        rebuilt_out(3, 0, "S")
+        rebuilt_out(4, 0, "S")
+        rebuilt(0, 1, (0, 1, 2))
+        rebuilt_out(5, 0, "S")
+        rebuilt_out(6, 0, "S")
+        hid_fold(0, "S")
+        rebuilt(1, 1, (0, 1, 2))
+        rebuilt_out(7, 0, "S")
+        hid_fold(1, "S")
+        g_quant(2, 0, 0)
+        rebuilt_out(0, 1, "S")
+        hid_fold(2, "S")
+        rebuilt(2, 1, (0, 1, 2))
+        hid_fold(3, "V")
+        rebuilt_out(1, 1, "S")
+        rebuilt(3, 1, (0, 1, 2))
+        hid_mul(4)
+        g_quant(2, 0, 1)
+        rebuilt_out(2, 1, "S")
+        rebuilt(4, 1, (0, 1, 2))
+        hid_turn(0, 0, "S")
+        rebuilt_out(3, 1, "S")
+        hid_turn(0, 1, "S")
+        g_quant(2, 1, 0)
+        hid_turn(1, 0, "V")
+        hid_turn(1, 1, "S")
+        hid_quant(0, 0)
+        rebuilt(5, 1, (0, 1, 2))
+        hid_quant(0, 1)
+        hid_quant(1, 0)
+        rebuilt_out(4, 1, "S")
+        hid_quant(1, 1)
+        g_quant(2, 1, 1)
+        rebuilt(6, 1, (0, 1, 2))
+        rebuilt_out(5, 1, "S")
+        hid_mul(5)
+        rebuilt(7, 1, (0, 1, 2))
+        rebuilt_out(6, 1, "S")
+        rebuilt_out(7, 1, "S")
+        hid_mul(6)
+        logits(0, 0, "S")
+        logits(1, 0, "S")
+        logits(2, 0, "V")
+        hid_mul(7)
+        hid_fold(4, "S")
+        hid_fold(5, "V")
+        logits(0, 1, "S")
+        logits(1, 1, "S")
+        logits(2, 1, "V")
+        hid_fold(6, "S")
+        hid_fold(7, "V")
+        logits(0, 2, "S")
+        logits(1, 2, "S")
+        logits(2, 2, "V")
+        hid_turn(2, 0, "S")
+        hid_quant(2, 0)
+        hid_turn(2, 1, "S")
+        hid_quant(2, 1)
+        hid_turn(3, 0, "V")
+        hid_turn(3, 1, "S")
+        hid_quant(3, 0)
+        logits(0, 3, "S")
+        logits(1, 3, "S")
+        logits(2, 3, "V")
+        hid_quant(3, 1)
+        logits(0, 4, "V")
+        logits(1, 4, "S")
+        logits(2, 4, "V")
+        logits(0, 5, "S")
+        logits(1, 5, "V")
+        logits(2, 5, "S")
+        logits(0, 6, "V")
+        logits(1, 6, "S")
+        logits(2, 6, "V")
+        logits(0, 7, "S")
+        logits(1, 7, "V")
+        logits(2, 7, "S")

from contextlib import ExitStack

import concourse.mybir as mybir
from concourse.masks import make_identity

F32 = mybir.dt.float32
BF16 = mybir.dt.bfloat16
I32 = mybir.dt.int32
U32 = mybir.dt.uint32
U8 = mybir.dt.uint8
FP8 = mybir.dt.float8_e4m3fn
FP8X4 = mybir.dt.float8_e4m3fn_x4
FP4X4 = mybir.dt.float4_e2m1fn_x4
MULT = mybir.AluOpType.mult
EXP = mybir.ActivationFunctionType.Exp
COPY = mybir.ActivationFunctionType.Copy

P = 128
PACK = 4
K, V, D, T = 1024, 1536, 1024, 1024
PASS = P * PACK
V_CHUNKS = V // PASS
K_PASSES = K // PASS
D_PASSES = D // PASS
T_TILES = T // P
K_TILES = K // P
FLOPS = 2 * V * K * D + 2 * T * D * V + 2 * K * V * D


def tile_tokenizer_swap_embed_s8_kernel(
    tc, sim, prior, emb, rnorm, hid_bytes, hid_scale, back_words, back_scales, out_0, out_1
):
    nc = tc.nc
    with ExitStack() as ctx:
        const = ctx.enter_context(tc.tile_pool(name="const", bufs=1))
        work = ctx.enter_context(tc.tile_pool(name="work", bufs=3))
        turn_psum = ctx.enter_context(tc.psum_pool(name="turn_psum", bufs=3))
        mx_psum = ctx.enter_context(tc.psum_pool(name="mx_psum", bufs=5))
        ctx.enter_context(tc.manual_schedule())

        ident = const.tile([P, P], F32, name="ident")
        make_identity(nc, ident[:])
        ident_bf = const.tile([P, P], BF16, name="ident_bf")
        make_identity(nc, ident_bf[:])
        warm = const.tile([P, 1], F32, name="warm")
        nc.vector.memset(warm[:], 0.0)
        nc.scalar.activation(out=warm[:], in_=warm[:], func=EXP)

        prior_sb = const.tile([P, K_PASSES, PACK], BF16, name="prior_sb")
        rnorm_bf = const.tile([P, V_CHUNKS, PACK], BF16, name="rnorm_bf")
        rnorm_sb = const.tile([P, V_CHUNKS * PACK], F32, name="rnorm_sb")

        def load_prior():
            nc.sync.dma_start(out=prior_sb[:], in_=prior.rearrange("(g p t) -> p g t", p=P, t=PACK))

        def load_rnorm():
            nc.sync.dma_start(out=rnorm_bf[:], in_=rnorm.rearrange("(h m t) -> m h t", m=P, t=PACK))
            nc.gpsimd.tensor_copy(out=rnorm_sb[:], in_=rnorm_bf[:].rearrange("m h t -> m (h t)"))

        sim_sb, emb_sb = {}, {}

        def load_sim(h, tp):
            sim_t = work.tile([P, 2, K], BF16, name="sim_t", bufs=4)
            src = sim[PASS * h : PASS * (h + 1), :].rearrange("(m t) k -> m t k", t=PACK)
            nc.sync.dma_start(out=sim_t[:], in_=src[:, 2 * tp : 2 * tp + 2, :])
            sim_sb[h, tp] = sim_t

        def load_emb(g, dh):
            emb_t = work.tile([P, PACK, PASS], BF16, name="emb_t", tag="big", bufs=4)
            src = emb[PASS * g : PASS * (g + 1), :].rearrange("(p j) d -> p j d", j=PACK)
            nc.sync.dma_start(out=emb_t[:], in_=src[:, :, PASS * dh : PASS * (dh + 1)])
            emb_sb[g, dh] = emb_t

        scale_sb = const.tile([P, D], F32, name="scale_sb")
        hid_codes_in = const.tile([P, T_TILES, D], U8, name="hid_codes_in")
        b_words = const.tile([P, V_CHUNKS, 2 * K], U8, name="b_words", align_bytes=64)
        b_scales = const.tile([P, V_CHUNKS, K], U8, name="b_scales", align_bytes=64)
        nc.gpsimd.memset(b_scales[:].rearrange("p h k -> p (h k)").bitcast(I32), 0)

        def load_hid(half):
            t4 = T_TILES // 2
            src = hid_bytes.rearrange("(r T) d -> r T d", T=T_TILES)
            nc.sync.dma_start(out=hid_codes_in[:, t4 * half : t4 * (half + 1), :], in_=src[:, t4 * half : t4 * (half + 1), :])

        def load_back():
            nc.sync.dma_start(out=b_words[:], in_=back_words.rearrange("h p w -> p h w"))
            src = back_scales.bitcast(I32).rearrange("h q k -> q h k")
            for q in range(4):
                nc.sync.dma_start(
                    out=b_scales[32 * q : 32 * q + 4, :, :].bitcast(I32), in_=src[4 * q : 4 * q + 4, :, :]
                )

        load_sim(0, 0)
        load_prior()
        load_emb(0, 0)
        load_sim(0, 1)
        load_emb(1, 0)
        load_emb(0, 1)
        load_emb(1, 1)
        load_rnorm()
        for tp in range(2):
            load_sim(1, tp)

        emb_codes = const.tile([P, K_PASSES, D], U32, name="emb_codes", align_bytes=64)
        emb_planes = const.tile([P, K_PASSES, D], U8, name="emb_planes", align_bytes=64)
        hid_codes = const.tile([P, D_PASSES, T], U32, name="hid_codes", align_bytes=64)
        hid_planes = const.tile([P, D_PASSES, T], U8, name="hid_planes", align_bytes=64)
        h_codes = const.tile([P, V_CHUNKS, D], U32, name="h_codes", align_bytes=64)
        h_planes = const.tile([P, V_CHUNKS, D], U8, name="h_planes", align_bytes=64)
        a_codes, a_planes, g_codes, g_planes = {}, {}, {}, {}
        def a_tiles(h):
            a_codes[h] = work.tile([P, K_PASSES, PASS], U32, name="a_codes", bufs=3, align_bytes=64)
            a_planes[h] = work.tile([P, K_PASSES, PASS], U8, name="a_planes", bufs=3, align_bytes=64)

        for h in range(V_CHUNKS):
            g_codes[h] = const.tile([P, D_PASSES, PASS], U32, name=f"g_codes_{h}", align_bytes=64)
            g_planes[h] = const.tile([P, D_PASSES, PASS], U8, name=f"g_planes_{h}", align_bytes=64)

        def late_loads():
            for tp in range(2):
                load_sim(2, tp)
            load_back()
            load_hid(0)
            load_hid(1)
            nc.sync.dma_start(out=scale_sb[:], in_=hid_scale.rearrange("o k -> (o k)").partition_broadcast(P))

        copiers = {"S": nc.scalar.copy, "V": nc.vector.tensor_copy}
        tiles = {}

        def quantize(src, codes, planes):
            nc.vector.quantize_mx(out=codes.bitcast(FP8X4), scales=planes, in_=src[:].rearrange("p c t -> p (c t)"))

        def sim_turn(h, tp, g):
            bank = turn_psum.tile([P, PASS], F32, name="turn")
            for tt in range(2):
                words = sim_sb[h, tp][:, tt, :].bitcast(F32)
                for u in range(2):
                    nc.tensor.transpose(
                        bank[:, 256 * u + P * tt : 256 * u + P * (tt + 1)], words[:, 256 * g + u : 256 * (g + 1) : 2], ident[:]
                    )
            ex = work.tile([P, 256, PACK], F32, name="ex", bufs=5)
            nc.scalar.activation(
                out=ex[:].rearrange("p c (u e) -> p c u e", u=2),
                in_=bank[:].bitcast(BF16).rearrange("p (u c e) -> p c u e", u=2, e=2),
                func=EXP,
            )
            tiles["ex", h, tp, g] = ex

        def a_mul(h, tp, g):
            ag = work.tile([P, 256, PACK], BF16, name="ag", align_bytes=64)
            nc.vector.tensor_tensor(
                out=ag[:],
                in0=tiles["ex", h, tp, g][:],
                in1=prior_sb[:, g, :].unsqueeze(1).to_broadcast([P, 256, PACK]),
                op=MULT,
            )
            tiles["ag", h, tp, g] = ag

        def a_quant(h, tp, g):
            if h not in a_codes:
                a_tiles(h)
            cols = slice(256 * tp, 256 * (tp + 1))
            quantize(tiles["ag", h, tp, g], a_codes[h][:, g, cols], a_planes[h][:, g, cols])

        def emb_group(g, dh, eng):
            eg = work.tile([P, PASS, PACK], BF16, name="eg", tag="grp", bufs=4, align_bytes=64)
            copiers[eng](
                out=eg[:].rearrange("p (c i) t -> p c t i", i=4), in_=emb_sb[g, dh][:].rearrange("p t (c i) -> p c t i", i=4)
            )
            tiles["eg", g, dh] = eg

        def emb_turn(g, dh, half, eng):
            bank = turn_psum.tile([P, 2 * P * PACK], BF16, name="turn_bf", tag="turn")
            for n in range(2):
                d0 = 2 * P * half + P * n
                nc.tensor.matmul(
                    out=bank[:, PASS * n : PASS * (n + 1)],
                    lhsT=ident_bf[:],
                    rhs=emb_sb[g, dh][:, :, d0 : d0 + P].rearrange("p t d -> p d t"),
                    start=True,
                    stop=True,
                )
            if ("eg", g, dh) not in tiles:
                eg = work.tile([P, PASS, PACK], BF16, name="eg", tag="grp", bufs=4, align_bytes=64)
                tiles["eg", g, dh] = eg
            copiers[eng](
                out=tiles["eg", g, dh][:, 2 * P * half : 2 * P * (half + 1), :].rearrange("p d t -> p (d t)"), in_=bank[:]
            )

        def emb_quant2(g, dh):
            emb_quant(g, dh)

        def emb_quant(g, dh):
            cols = slice(PASS * dh, PASS * (dh + 1))
            quantize(tiles["eg", g, dh], emb_codes[:, g, cols], emb_planes[:, g, cols])

        def hid_mul(i):
            hs = work.tile([P, D], BF16, name="hs", bufs=4)
            nc.vector.tensor_tensor(out=hs[:], in0=hid_codes_in[:, i, :].bitcast(FP8), in1=scale_sb[:], op=MULT)
            tiles["hs", i] = hs

        def hid_fold(i, eng):
            hf = work.tile([P, D_PASSES, 2, P], F32, name="hf", bufs=5)
            copiers[eng](
                out=hf[:].rearrange("r g u p -> r g u p"),
                in_=tiles["hs", i][:].bitcast(F32).rearrange("r (g p u) -> r g u p", g=D_PASSES, u=2),
            )
            tiles["hf", i] = hf

        def hid_turn(pair, g, eng):
            bank = turn_psum.tile([P, PASS], F32, name="turn")
            for tt in range(2):
                for u in range(2):
                    nc.tensor.transpose(
                        bank[:, 256 * u + P * tt : 256 * u + P * (tt + 1)], tiles["hf", 2 * pair + tt][:, g, u, :], ident[:]
                    )
            hg = work.tile([P, 256, PACK], BF16, name="hidg", bufs=4, align_bytes=64)
            copiers[eng](
                out=hg[:].rearrange("p c t -> p (c t)").bitcast(F32).rearrange("p (c u) -> p c u", u=2),
                in_=bank[:].rearrange("p (u c) -> p c u", u=2),
            )
            tiles["hidg", pair, g] = hg

        def hid_quant(pair, g):
            cols = slice(256 * pair, 256 * (pair + 1))
            quantize(tiles["hidg", pair, g], hid_codes[:, g, cols], hid_planes[:, g, cols])

        def e_mm(h, t, dh, eng="S"):
            acc = mx_psum.tile([P, PASS], F32, name="acc")
            rows, cols = slice(P * t, P * (t + 1)), slice(PASS * dh, PASS * (dh + 1))
            for g in range(K_PASSES):
                nc.tensor.matmul_mx(
                    out=acc[:],
                    lhsT=a_codes[h][:, g, rows].bitcast(FP8X4),
                    lhsT_scale=a_planes[h][:, g, rows],
                    rhs=emb_codes[:, g, cols].bitcast(FP8X4),
                    rhs_scale=emb_planes[:, g, cols],
                    start=(g == 0),
                    stop=(g == K_PASSES - 1),
                )
            if ("ep", h, dh) not in tiles:
                ep = work.tile([P, PACK, PASS], BF16, name=f"ep{dh}", bufs=3)
                tiles["ep", h, dh] = ep
            planes = tiles["ep", h, dh][:, t, :].rearrange("m (u p e) -> m u p e", u=2, e=2)
            sums = acc[:].rearrange("m (p u e) -> m u p e", u=2, e=2)
            norm = rnorm_sb[:, PACK * h + t : PACK * h + t + 1]
            if eng == "S":
                nc.scalar.activation(out=planes, in_=sums, func=COPY, scale=norm)
            else:
                nc.vector.tensor_scalar(out=planes, in0=sums, scalar1=norm, scalar2=None, op0=MULT)

        def h_group(h, dh, eng="V"):
            hg = work.tile([P, PASS, PACK], BF16, name="hg", tag="grp", bufs=4, align_bytes=64)
            copiers[eng](
                out=hg[:].rearrange("p (c i) t -> p c t i", i=4), in_=tiles["ep", h, dh][:].rearrange("p t (c i) -> p c t i", i=4)
            )
            tiles["hg", h, dh] = hg

        def h_quant(h, dh):
            cols = slice(PASS * dh, PASS * (dh + 1))
            quantize(tiles["hg", h, dh], h_codes[:, h, cols], h_planes[:, h, cols])

        def e_turn(h, dh, tp, eng):
            bank = turn_psum.tile([P, PASS], F32, name="turn")
            for tt in range(2):
                words = tiles["ep", h, dh][:, 2 * tp + tt, :].bitcast(F32)
                for u in range(2):
                    nc.tensor.transpose(
                        bank[:, 256 * u + P * tt : 256 * u + P * (tt + 1)], words[:, P * u : P * (u + 1)], ident[:]
                    )
            gg = work.tile([P, 256, PACK], BF16, name="gg", align_bytes=64, bufs=6)
            copiers[eng](
                out=gg[:].rearrange("p c t -> p (c t)").bitcast(F32).rearrange("p (c u) -> p c u", u=2),
                in_=bank[:].rearrange("p (u c) -> p c u", u=2),
            )
            tiles["gg", h, dh, tp] = gg

        def g_quant(h, dh, tp):
            cols = slice(256 * tp, 256 * (tp + 1))
            quantize(tiles["gg", h, dh, tp], g_codes[h][:, dh, cols], g_planes[h][:, dh, cols])

        def logits(h, i, eng):
            acc = mx_psum.tile([P, PASS], F32, name="acc")
            cols = slice(P * i, P * (i + 1))
            for g in range(D_PASSES):
                nc.tensor.matmul_mx(
                    out=acc[:],
                    lhsT=hid_codes[:, g, cols].bitcast(FP8X4),
                    lhsT_scale=hid_planes[:, g, cols],
                    rhs=g_codes[h][:, g, :].bitcast(FP8X4),
                    rhs_scale=g_planes[h][:, g, :],
                    start=(g == 0),
                    stop=(g == D_PASSES - 1),
                )
            if ("lo", i) not in tiles:
                lo = work.tile([P, V], F32, name="lo", tag="big", bufs=4)
                tiles["lo", i] = lo
            cols = slice(PASS * h, PASS * (h + 1))
            piece = tiles["lo", i][:, cols]
            copiers[eng](out=piece.rearrange("r (m t) -> r m t", t=PACK), in_=acc[:].rearrange("r (t m) -> r m t", t=PACK))
            dst = out_0.rearrange("(r T) v -> T r v", T=T_TILES)[i]
            if i == T_TILES - 1:
                nc.sync.dma_start(out=dst[:, cols], in_=piece)
            elif h == V_CHUNKS - 1:
                nc.sync.dma_start(out=dst, in_=tiles["lo", i][:])

        def rebuilt(i, dh, chunks):
            if chunks[0] == 0:
                tiles["reb", i, dh] = mx_psum.tile([P, PASS], F32, name="acc")
            cols = slice(PASS * dh, PASS * (dh + 1))
            for h in chunks:
                nc.tensor.matmul_mx(
                    out=tiles["reb", i, dh][:],
                    lhsT=b_words[:, h, 2 * P * i : 2 * P * (i + 1)].bitcast(FP4X4),
                    lhsT_scale=b_scales[:, h, P * i : P * (i + 1)],
                    rhs=h_codes[:, h, cols].bitcast(FP8X4),
                    rhs_scale=h_planes[:, h, cols],
                    start=(h == 0),
                    stop=(h == V_CHUNKS - 1),
                )

        def rebuilt_out(i, dh, eng):
            cols = slice(PASS * dh, PASS * (dh + 1))
            ro = work.tile([P, PASS], F32, name="ro", bufs=4)
            copiers[eng](
                out=ro[:].rearrange("k (p u e) -> k p u e", u=2, e=2),
                in_=tiles["reb", i, dh][:].rearrange("k (u p e) -> k p u e", u=2, e=2),
            )
            nc.sync.dma_start(out=out_1[P * i : P * (i + 1), cols], in_=ro[:])

        emb_group(0, 0, "V")
        sim_turn(0, 0, 0)
        a_mul(0, 0, 0)
        sim_turn(0, 0, 1)
        sim_turn(0, 1, 0)
        a_mul(0, 0, 1)
        sim_turn(0, 1, 1)
        late_loads()
        a_quant(0, 0, 0)
        a_mul(0, 1, 0)
        emb_group(1, 0, "V")
        a_mul(0, 1, 1)
        emb_group(0, 1, "S")
        a_quant(0, 0, 1)
        emb_group(1, 1, "V")
        a_quant(0, 1, 0)
        emb_quant(0, 0)
        sim_turn(1, 0, 0)
        emb_quant(1, 0)
        sim_turn(1, 0, 1)
        sim_turn(1, 1, 0)
        sim_turn(1, 1, 1)
        a_quant(0, 1, 1)
        emb_quant(0, 1)
        a_mul(1, 0, 0)
        a_mul(1, 0, 1)
        emb_quant(1, 1)
        a_mul(1, 1, 0)
        sim_turn(2, 0, 0)
        a_quant(1, 0, 0)
        a_quant(1, 0, 1)
        a_mul(1, 1, 1)
        sim_turn(2, 0, 1)
        a_quant(1, 1, 0)
        a_quant(1, 1, 1)
        e_mm(0, 0, 0, "S")
        sim_turn(2, 1, 0)
        e_mm(0, 1, 0, "S")
        sim_turn(2, 1, 1)
        e_mm(0, 2, 0, "V")
        e_mm(0, 3, 0, "S")
        a_mul(2, 0, 0)
        e_mm(0, 0, 1, "S")
        e_mm(0, 1, 1, "V")
        e_mm(0, 2, 1, "S")
        e_mm(0, 3, 1, "S")
        e_turn(0, 0, 0, "S")
        a_mul(2, 0, 1)
        e_turn(0, 0, 1, "S")
        e_turn(0, 1, 0, "S")
        e_turn(0, 1, 1, "V")
        a_mul(2, 1, 0)
        a_quant(2, 0, 0)
        a_quant(2, 0, 1)
        a_mul(2, 1, 1)
        a_quant(2, 1, 0)
        a_quant(2, 1, 1)
        e_mm(1, 0, 0, "S")
        e_mm(1, 1, 0, "S")
        e_mm(1, 2, 0, "S")
        e_mm(1, 3, 0, "S")
        e_mm(1, 0, 1, "S")
        e_mm(1, 1, 1, "S")
        e_mm(1, 2, 1, "S")
        h_group(0, 0, "V")
        h_group(0, 1, "V")
        e_mm(1, 3, 1, "S")
        g_quant(0, 0, 0)
        e_mm(2, 0, 0, "S")
        e_mm(2, 1, 0, "S")
        g_quant(0, 0, 1)
        h_group(1, 0, "V")
        e_turn(1, 0, 0, "S")
        e_mm(2, 2, 0, "S")
        e_turn(1, 0, 1, "S")
        e_turn(1, 1, 0, "V")
        e_turn(1, 1, 1, "S")
        e_mm(2, 3, 0, "S")
        e_mm(2, 0, 1, "S")
        g_quant(0, 1, 0)
        h_group(2, 0, "V")
        e_mm(2, 1, 1, "S")
        h_quant(1, 0)
        h_quant(0, 0)
        e_mm(2, 2, 1, "S")
        h_quant(2, 0)
        g_quant(1, 0, 0)
        e_mm(2, 3, 1, "S")
        g_quant(0, 1, 1)
        g_quant(1, 0, 1)
        h_group(2, 1, "V")
        g_quant(1, 1, 0)
        h_quant(0, 1)
        g_quant(1, 1, 1)
        h_group(1, 1, "V")
        e_turn(2, 0, 0, "S")
        h_quant(2, 1)
        e_turn(2, 0, 1, "S")
        h_quant(1, 1)
        e_turn(2, 1, 0, "S")
        hid_mul(0)
        hid_mul(1)
        hid_mul(2)
        hid_mul(3)
        e_turn(2, 1, 1, "S")
        rebuilt(0, 0, (0, 1, 2))
        rebuilt_out(0, 0, "S")
        rebuilt(1, 0, (0, 1, 2))
        rebuilt(2, 0, (0, 1, 2))
        rebuilt(3, 0, (0, 1, 2))
        rebuilt_out(1, 0, "S")
        rebuilt(4, 0, (0, 1, 2))
        rebuilt(5, 0, (0, 1, 2))
        rebuilt(6, 0, (0, 1, 2))
        rebuilt_out(2, 0, "S")
        rebuilt(7, 0, (0, 1, 2))
        rebuilt_out(3, 0, "S")
        rebuilt_out(4, 0, "S")
        rebuilt(0, 1, (0, 1, 2))
        rebuilt_out(5, 0, "S")
        rebuilt_out(6, 0, "S")
        hid_fold(0, "S")
        rebuilt(1, 1, (0, 1, 2))
        rebuilt_out(7, 0, "S")
        hid_fold(1, "S")
        g_quant(2, 0, 0)
        rebuilt_out(0, 1, "S")
        hid_fold(2, "S")
        rebuilt(2, 1, (0, 1, 2))
        hid_fold(3, "V")
        rebuilt_out(1, 1, "S")
        rebuilt(3, 1, (0, 1, 2))
        hid_mul(4)
        g_quant(2, 0, 1)
        rebuilt_out(2, 1, "S")
        rebuilt(4, 1, (0, 1, 2))
        hid_turn(0, 0, "S")
        rebuilt_out(3, 1, "S")
        hid_turn(0, 1, "S")
        g_quant(2, 1, 0)
        hid_turn(1, 0, "V")
        hid_turn(1, 1, "S")
        hid_quant(0, 0)
        rebuilt(5, 1, (0, 1, 2))
        hid_quant(0, 1)
        hid_quant(1, 0)
        rebuilt_out(4, 1, "S")
        hid_quant(1, 1)
        g_quant(2, 1, 1)
        rebuilt(6, 1, (0, 1, 2))
        rebuilt_out(5, 1, "S")
        hid_mul(5)
        rebuilt(7, 1, (0, 1, 2))
        rebuilt_out(6, 1, "S")
        rebuilt_out(7, 1, "S")
        hid_mul(6)
        logits(0, 0, "S")
        logits(1, 0, "S")
        logits(2, 0, "V")
        hid_mul(7)
        hid_fold(4, "S")
        hid_fold(5, "V")
        logits(0, 1, "S")
        logits(1, 1, "S")
        logits(2, 1, "V")
        hid_fold(6, "S")
        hid_fold(7, "V")
        logits(0, 2, "S")
        logits(1, 2, "S")
        logits(2, 2, "V")
        hid_turn(2, 0, "S")
        hid_quant(2, 0)
        hid_turn(2, 1, "S")
        hid_quant(2, 1)
        hid_turn(3, 0, "V")
        hid_turn(3, 1, "S")
        hid_quant(3, 0)
        logits(0, 3, "S")
        logits(1, 3, "S")
        logits(2, 3, "V")
        hid_quant(3, 1)
        logits(0, 4, "V")
        logits(1, 4, "S")
        logits(2, 4, "V")
        logits(0, 5, "S")
        logits(1, 5, "V")
        logits(2, 5, "S")
        logits(0, 6, "V")
        logits(1, 6, "S")
        logits(2, 6, "V")
        logits(0, 7, "S")
        logits(1, 7, "V")
        logits(2, 7, "S")
